import numpy as np
import ml_dtypes


def mxq(x, axis, fmt="e4m3"):
    dtype, down = {"e4m3": (ml_dtypes.float8_e4m3fn, 7), "e5m2": (ml_dtypes.float8_e5m2, 14)}[fmt]
    v = np.moveaxis(np.asarray(x, np.float32).astype(ml_dtypes.bfloat16).astype(np.float64), axis, -1)
    blocks = v.reshape(v.shape[:-1] + (-1, 32))
    amax = np.abs(blocks).max(-1, keepdims=True)
    byte = np.maximum(np.where(amax > 0, np.frexp(amax)[1] - 1 + 127, 0) - down, 1)
    scale = np.exp2(byte - 127.0)
    codes = (blocks / scale).astype(np.float32).astype(dtype).astype(np.float64)
    return np.moveaxis((codes * scale).reshape(v.shape), -1, axis)


WIDE = False


def mx_kscale(k):
    if not WIDE:
        return np.ones(k)
    levels = np.array([10, -10, 5, -5, 0])
    if k % 512:
        return np.exp2(np.random.permutation(np.resize(levels, k // 32))).repeat(32)
    a = np.empty((k // 512, 16))
    for p in range(k // 512):
        a[p, :8] = np.random.permutation(np.resize(levels, 8))
        for g in range(8):
            far = levels[np.abs(levels - a[p, g]) >= 10]
            a[p, g + 8] = far[np.random.randint(len(far))]
    return np.exp2(a.ravel()).repeat(32)


BF16 = ml_dtypes.bfloat16


def bf(x):
    return np.asarray(x, np.float32).astype(BF16)


def f64(x):
    return np.asarray(x).astype(np.float64)


E2M1 = np.array([0.0, 0.5, 1.0, 1.5, 2.0, 3.0, 4.0, 6.0, -0.0, -0.5, -1.0, -1.5, -2.0, -3.0, -4.0, -6.0])


def pack_weight(w, fmt):
    k, n = w.shape
    w = f64(bf(w)).reshape(k // 32, 32, n)
    amax = np.abs(w).max(1)
    if fmt == "e4m3":
        byte = np.frexp(amax)[1] - 1 + 127 - 7
    else:
        mant, ex = np.frexp(amax / 6.0)
        byte = np.where(mant > 0.5, ex, ex - 1) + 127
    byte = np.clip(np.where(amax > 0, byte, 1), 1, 254)
    scaled = (w * np.exp2(127.0 - byte)[:, None, :]).reshape(k, n).astype(np.float32)
    by_word = np.ascontiguousarray(scaled.reshape(k // 512, 128, 4, n).transpose(0, 1, 3, 2))
    if fmt == "e4m3":
        words = by_word.astype(ml_dtypes.float8_e4m3fn).view(np.uint8)
    else:
        c = by_word.astype(ml_dtypes.float4_e2m1fn).view(np.uint8) & 0xF
        words = c[..., 0::2] | (c[..., 1::2] << 4)
    return np.ascontiguousarray(words), np.ascontiguousarray(byte.astype(np.uint8).reshape(k // 512, 16, n))


def unpack_weight(words, scales, fmt):
    g, p, n, _ = words.shape
    if fmt == "e4m3":
        vals = np.ascontiguousarray(words).view(ml_dtypes.float8_e4m3fn).astype(np.float64)
    else:
        nib = np.empty((g, p, n, 4), np.uint8)
        nib[..., 0::2] = words & 0xF
        nib[..., 1::2] = words >> 4
        vals = E2M1[nib]
    vals = vals * np.repeat(np.exp2(scales.astype(np.float64) - 127.0), 8, axis=1)[..., None]
    return vals.transpose(0, 1, 3, 2).reshape(g * 512, n)
def pack4(w):
    words, scales = pack_weight(w, "e2m1")
    return words.reshape(words.shape[0], 128, -1), scales


def unpack4(words, scales):
    return unpack_weight(words.reshape(words.shape[0], 128, -1, 2), scales, "e2m1")


def planes(Y):
    n, m = Y.shape
    b = f64(bf(Y)).reshape(n // 32, 32, m)
    amax = np.abs(b).max(1)
    byte = np.clip(np.where(amax > 0, np.frexp(amax)[1] - 1 + 127 - 7, 1), 1, 254)
    codes = (b * np.exp2(127.0 - byte)[:, None, :]).reshape(n, m).astype(np.float32).astype(ml_dtypes.float8_e4m3fn).view(np.uint8)
    words = codes.reshape(n // 512, 128, 4, m).transpose(0, 1, 3, 2)
    return np.ascontiguousarray(words), np.ascontiguousarray(byte.astype(np.uint8).reshape(n // 512, 16, m))


N, D, F, O, T = 1024, 1024, 1024, 512, 3


def normalized_hermite(u):
    u2 = u * u
    u3 = u2 * u
    h1 = u
    h2 = (u2 - 1.0) / np.sqrt(2.0)
    h3 = (u3 - 3.0 * u) / np.sqrt(6.0)
    return h1, h2, h3


def setup_inputs():
    s = mx_kscale(D)
    t = np.stack([mx_kscale(F) for _ in range(T)])
    x = bf(np.random.standard_normal((N, D)) * s)
    words, scales = pack4(np.random.standard_normal((D, F)) / np.sqrt(D) / s[:, None])
    return {"x": x,
            "w_words": words,
            "w_scales": scales,
            "g": bf((1.0 + 0.1 * np.random.standard_normal((T, F))) * t),
            "c": bf(np.random.standard_normal((T, F, O)) / np.sqrt(F) / t[:, :, None]),
            "b": bf(np.random.standard_normal(O) * 0.5)}


def core(x, w_words, w_scales, g, c, b):
    g, c = f64(g), f64(c)
    u = mxq(f64(x), 1, "e4m3") @ unpack4(w_words, w_scales)
    h1, h2, h3 = normalized_hermite(u)
    k1 = h1 * g[0]
    k2 = h2 * g[1]
    k3 = h3 * g[2]
    y1 = mxq(k1, 1, "e4m3") @ mxq(c[0], 0, "e4m3")
    y2 = mxq(k2, 1, "e4m3") @ mxq(c[1], 0, "e4m3")
    y3 = mxq(k3, 1, "e4m3") @ mxq(c[2], 0, "e4m3")
    return y1 + y2 + y3 + f64(b)


def reference(x, w_words, w_scales, g, c, b):
    R_out = core(x, w_words, w_scales, g, c, b)
    words, scales = planes(R_out.T)
    return R_out, words, scales

@@ -1,0 +1,411 @@
+import math
+from contextlib import ExitStack
+
+import concourse.mybir as mybir
+from concourse.masks import make_identity
+
+N, D, F, O = 1024, 1024, 1024, 512
+FLOPS = 2 * N * D * F + 3 * 2 * N * F * O
+
+F32 = mybir.dt.float32
+BF16 = mybir.dt.bfloat16
+U32 = mybir.dt.uint32
+I32 = mybir.dt.int32
+U8 = mybir.dt.uint8
+FP8X4 = mybir.dt.float8_e4m3fn_x4
+FP4X4 = mybir.dt.float4_e2m1fn_x4
+ALU = mybir.AluOpType
+ACT = mybir.ActivationFunctionType
+
+P = 128
+TILES = N // P
+
+C_ENGINE = ["VS","VS","VS","VS","SS","SS"]
+C_STEP = {0: -1, 1: -1, 2: 1, 3: 4, 4: 2, 5: 4}
+K1S = {7, 8, 10, 12, 13, 14}
+Y_STEP = {}
+Y_AT = {5: 0, 7: 1, 8: 2, 9: 3, 10: 4, 12: 5, 15: 6}
+
+
+def tile_hermitechaosridgeexpansiondegreethree_x2_kernel(tc, x, w_words, w_scales, g, c, b, out_0, out_1, out_2):
+    nc = tc.nc
+    with ExitStack() as ctx:
+        keep = ctx.enter_context(tc.tile_pool(name="keep", bufs=1))
+        work = ctx.enter_context(tc.tile_pool(name="work", bufs=3))
+        psum = ctx.enter_context(tc.psum_pool(name="psum", bufs=1))
+
+        ident = keep.tile([P, P], F32, align_bytes=64, name="ident")
+        g_rows = keep.tile([P, 512], BF16, align_bytes=64, name="g_rows")
+        g_perm = keep.tile([P, 4, 128], F32, align_bytes=64, name="g_perm")
+        gains = keep.tile([P, 4, 2, 4], F32, align_bytes=64, name="gains")
+        ws_raw = keep.tile([P, 2, 1024], U8, align_bytes=64, name="ws_raw")
+        ws = keep.tile([P, 2, 2, 4, 128], U8, align_bytes=64, name="ws")
+        w_raw = keep.tile([P, 2, 2, 1024], U8, align_bytes=64, name="w_raw")
+        wc = keep.tile([P, 2, 2, 4, 256], U8, align_bytes=64, name="wc")
+        x_codes = keep.tile([P, TILES, 2, 128], U32, align_bytes=64, name="x_codes")
+        x_scales = keep.tile([P, TILES, 2, 128], U8, align_bytes=64, name="x_scales")
+        c_raw = keep.tile([P, 6, 4, 512], BF16, align_bytes=64, name="c_raw")
+        c_codes = keep.tile([P, 6, 512], U32, align_bytes=64, name="c_codes")
+        c_scales = keep.tile([P, 6, 512], U8, align_bytes=64, name="c_scales")
+        bias = keep.tile([P, 512], BF16, align_bytes=64, name="bias")
+        y_codes = keep.tile([P, N], U32, align_bytes=64, name="y_codes")
+        y_scales = keep.tile([P, N], U8, align_bytes=64, name="y_scales")
+        warm = keep.tile([P, 1], F32, align_bytes=64, name="warm")
+
+        nc.vector.memset(g_rows[:].bitcast(I32), 0)
+        nc.vector.memset(ws_raw[:].rearrange("p g n -> p (g n)").bitcast(I32), 0)
+        nc.sync.dma_start(out=g_rows[0:6, :], in_=g.rearrange("d (h f) -> (d h) f", h=2))
+        xs = []
+        for i in range(TILES):
+            x_sb = keep.tile([P, D], BF16, align_bytes=64, name="x_sb%d" % i)
+            xs.append(x_sb)
+
+        def load_x(i):
+            nc.sync.dma_start(out=xs[i][:], in_=x[128 * i : 128 * (i + 1), :])
+
+        def load_c(j):
+            rows = c[j // 2, 512 * (j % 2) : 512 * (j % 2 + 1), :].rearrange("(B t e) o -> t B e o", t=4, e=8)
+            for t in range(4):
+                nc.sync.dma_start(out=c_raw[:, j, t, :], in_=rows[t])
+
+        def load_w(fg):
+            half = slice(1024 * fg, 1024 * (fg + 1))
+            nc.sync.dma_start(
+                out=w_raw[:, fg, :, :].bitcast(I32), in_=w_words[:, :, half].rearrange("g p n -> p g n").bitcast(I32)
+            )
+
+        load_x(0)
+        load_w(0)
+        for q in range(4):
+            nc.scalar.dma_start(
+                out=ws_raw[32 * q : 32 * q + 4, :, :].bitcast(I32),
+                in_=w_scales[:, 4 * q : 4 * q + 4, :].rearrange("g q n -> q g n").bitcast(I32),
+            )
+        load_x(1)
+        load_w(1)
+        load_c(0)
+        load_c(1)
+        load_x(2)
+        load_c(2)
+        load_c(3)
+        load_x(3)
+        load_c(4)
+        load_c(5)
+        nc.sync.dma_start(out=bias[:], in_=b.partition_broadcast(P))
+        for i in range(4, TILES):
+            load_x(i)
+
+        make_identity(nc, ident[:])
+        nc.vector.memset(warm[:], 0.0)
+        nc.scalar.activation(out=warm[:], in_=warm[:], func=ACT.Square)
+
+        nc.vector.tensor_copy(
+            out=g_perm[:].rearrange("p t (B e) -> p t B e", e=8),
+            in_=g_rows[:].rearrange("p (B t e) -> p t B e", t=4, e=8),
+        )
+        gt = psum.tile([P, 4, 128], F32, tag="turn", bufs=2, name="gt")
+        for t in range(4):
+            nc.tensor.transpose(gt[:, t, :], g_perm[:, t, :], ident[:])
+
+        def make_gains():
+          for k, (d, f) in enumerate([(0, 1.0), (1, 1.0 / math.sqrt(2.0)), (2, 1.0 / math.sqrt(6.0)), (2, -3.0 / math.sqrt(6.0))]):
+              nc.vector.tensor_scalar_mul(gains[:, k, :, :], gt[:, :, 2 * d : 2 * d + 2].rearrange("p t r -> p r t"), f)
+
+        x_groups = {}
+
+        x_banks = {}
+
+        def x_turn(i):
+            words = xs[i][:].bitcast(F32)
+            xt = psum.tile([P, 4, 128], F32, tag="turn", bufs=2, name="xt")
+            for kg in range(2):
+                for u in range(2):
+                    nc.tensor.transpose(xt[:, 2 * kg + u, :], words[:, 256 * kg + u : 256 * (kg + 1) : 2], ident[:])
+            x_banks[i] = xt
+
+        def x_out(i):
+            xt = x_banks[i]
+            x_grp = work.tile([P, 2 * 128 * 4], BF16, align_bytes=64, name="x_grp")
+            nc.scalar.copy(
+                out=x_grp[:].bitcast(F32).rearrange("p (k r u) -> p k r u", k=2, u=2),
+                in_=xt[:].rearrange("p (k u) r -> p k r u", u=2),
+            )
+            x_groups[i] = x_grp
+
+        def x_quant(i):
+            nc.vector.quantize_mx(
+                out=x_codes[:, i, :, :].rearrange("p k n -> p (k n)").bitcast(FP8X4),
+                scales=x_scales[:, i, :, :].rearrange("p k n -> p (k n)"),
+                in_=x_groups[i][:],
+            )
+
+        def w_perm(fg):
+            for kg in range(2):
+                nc.vector.tensor_copy(
+                    out=wc[:, fg, kg, :, :].bitcast(I32).rearrange("p t (B e) -> p t B e", e=4),
+                    in_=w_raw[:, fg, kg, :].bitcast(I32).rearrange("p (B t e) -> p t B e", t=4, e=4),
+                )
+                nc.vector.tensor_copy(
+                    out=ws[:, fg, kg, :, :].bitcast(I32).rearrange("p t (B e) -> p t B e", e=2),
+                    in_=ws_raw[:, kg, 512 * fg : 512 * (fg + 1)].bitcast(I32).rearrange("p (B t e) -> p t B e", t=4, e=2),
+                )
+
+        c_groups = {}
+
+        def c_interleave(j, h):
+                if h == 0:
+                    c_grp_new = work.tile([P, 512, 4], BF16, align_bytes=64, name="c_grp_new")
+                    c_groups[j] = c_grp_new
+                c_grp = c_groups[j]
+                o = slice(256 * h, 256 * (h + 1))
+                dst = c_grp[:, o, :].rearrange("p (c i) t -> p c t i", i=4)
+                src = c_raw[:, j, :, o].rearrange("p t (c i) -> p c t i", i=4)
+                who = C_ENGINE[j][h]
+                if who == "V":
+                    nc.vector.tensor_copy(out=dst, in_=src)
+                elif who == "S":
+                    nc.scalar.copy(out=dst, in_=src)
+                else:
+                    nc.gpsimd.tensor_scalar(out=dst, in0=src, scalar1=1.0, scalar2=0.0, op0=ALU.mult, op1=ALU.add)
+
+        def c_quant(j):
+            nc.vector.quantize_mx(
+                out=c_codes[:, j, :].bitcast(FP8X4),
+                scales=c_scales[:, j, :],
+                in_=c_groups[j][:].rearrange("p o t -> p (o t)"),
+            )
+
+        u_banks = {}
+        squares = {}
+        thirds = {}
+        ka = {}
+        kb = {}
+        k_codes = {}
+        y_banks = {}
+        y_sbs = {}
+        y_groups = {}
+        y_turned = {}
+        k1_slots = {}
+
+        def s_k1(n):
+            fg = n % 2
+            k1_slot = work.tile([P, 4, 128], BF16, align_bytes=64, name="k1_slot")
+            for t in range(4):
+                nc.scalar.activation(
+                    out=k1_slot[:, t, :], in_=u_banks[n][:, t, :], func=ACT.Copy, scale=gains[:, 0, fg, t : t + 1]
+                )
+            k1_slots[n] = k1_slot
+
+        def s_k1b(n):
+            i, fg = divmod(n, 2)
+            nc.scalar.copy(out=ka[i][:, fg, 0, :, :], in_=k1_slots[n][:].rearrange("p t n -> p n t"))
+
+        def u_mm(n):
+            i, fg = divmod(n, 2)
+            u = psum.tile([P, 4, 128], F32, tag="u", bufs=4, name="u")
+            for t in range(4):
+                for kg in range(2):
+                    nc.tensor.matmul_mx(
+                        out=u[:, t, :],
+                        lhsT=wc[:, fg, kg, t, :].bitcast(FP4X4),
+                        lhsT_scale=ws[:, fg, kg, t, :],
+                        rhs=x_codes[:, i, kg, :].bitcast(FP8X4),
+                        rhs_scale=x_scales[:, i, kg, :],
+                        start=(kg == 0),
+                        stop=(kg == 1),
+                    )
+            u_banks[n] = u
+
+        def s_square(n):
+            u2 = work.tile([P, 4, 128], F32, align_bytes=64, name="u2")
+            nc.scalar.activation(out=u2[:], in_=u_banks[n][:], func=ACT.Square)
+            squares[n] = u2
+
+        def s_third(n):
+            z = work.tile([P, 4, 128], F32, align_bytes=64, name="z")
+            for t in range(4):
+                nc.scalar.activation(
+                    out=z[:, t, :],
+                    in_=squares[n][:, t, :],
+                    func=ACT.Identity,
+                    scale=gains[:, 2, n % 2, t : t + 1],
+                    bias=gains[:, 3, n % 2, t : t + 1],
+                )
+            thirds[n] = z
+
+        def spread(k, fg):
+            return gains[:, k, fg, :].unsqueeze(1).to_broadcast([P, 128, 4])
+
+        def k_tiles(n):
+            i, fg = divmod(n, 2)
+            if fg == 0:
+                ka_t = work.tile([P, 2, 2, 128, 4], BF16, align_bytes=64, name="ka_t")
+                kb_t = work.tile([P, 2, 128, 4], BF16, align_bytes=64, name="kb_t")
+                ka[i] = ka_t
+                kb[i] = kb_t
+
+        def v_k2(n):
+            i, fg = divmod(n, 2)
+            nc.vector.scalar_tensor_tensor(
+                out=ka[i][:, fg, 1, :, :],
+                in0=squares[n][:].rearrange("p t n -> p n t"),
+                scalar=-1.0,
+                in1=spread(1, fg),
+                op0=ALU.add,
+                op1=ALU.mult,
+            )
+
+        def v_k1(n):
+            i, fg = divmod(n, 2)
+            nc.vector.tensor_tensor(
+                out=ka[i][:, fg, 0, :, :], in0=u_banks[n][:].rearrange("p t n -> p n t"), in1=spread(0, fg), op=ALU.mult
+            )
+
+        def v_k3(n):
+            i, fg = divmod(n, 2)
+            nc.vector.tensor_tensor(
+                out=kb[i][:, fg, :, :],
+                in0=u_banks[n][:].rearrange("p t n -> p n t"),
+                in1=thirds[n][:].rearrange("p t n -> p n t"),
+                op=ALU.mult,
+            )
+
+        def k_codes_tiles(i):
+            kc = keep.tile([P, 6, 128], U32, align_bytes=64, name="kc%d" % i)
+            ks = keep.tile([P, 6, 128], U8, align_bytes=64, name="ks%d" % i)
+            k_codes[i] = (kc, ks)
+
+        def k_quant_part(i, a, z, src):
+            kc, ks = k_codes[i]
+            nc.vector.quantize_mx(
+                out=kc[:, a:z, :].rearrange("p j n -> p (j n)").bitcast(FP8X4),
+                scales=ks[:, a:z, :].rearrange("p j n -> p (j n)"),
+                in_=src,
+            )
+
+        def k_quant(i):
+            k_codes_tiles(i)
+            k_quant_part(i, 0, 4, ka[i][:].rearrange("p f d n t -> p (f d n t)"))
+            k_quant_part(i, 4, 6, kb[i][:].rearrange("p f n t -> p (f n t)"))
+
+        def y_pass(i, a, j, s):
+            kc, ks = k_codes[i]
+            nc.tensor.matmul_mx(
+                out=y_banks[i][:],
+                lhsT=kc[:, s, :].bitcast(FP8X4),
+                lhsT_scale=ks[:, s, :],
+                rhs=c_codes[:, j, :].bitcast(FP8X4),
+                rhs_scale=c_scales[:, j, :],
+                start=(a == 0),
+                stop=(a == 5),
+            )
+
+        def y_bank(i):
+            y = psum.tile([P, 512], F32, tag="y", bufs=2, name="y")
+            y_banks[i] = y
+
+        PASSES = [(0, 0), (2, 1), (4, 4), (1, 2), (3, 3), (5, 5)]
+
+        def y_mm(i):
+            y_bank(i)
+            for a, (j, s) in enumerate(PASSES):
+                y_pass(i, a, j, s)
+
+        def v_y(i):
+            y_sb = work.tile([P, 512], F32, align_bytes=64, name="y_sb")
+            nc.vector.tensor_tensor(out=y_sb[:], in0=y_banks[i][:], in1=bias[:], op=ALU.add)
+            nc.sync.dma_start(out=out_0[128 * i : 128 * (i + 1), :], in_=y_sb[:])
+            y_sbs[i] = y_sb
+
+        def y_turn(i):
+            yt = psum.tile([P, 4, 128], F32, tag="turn", bufs=2, name="yt")
+            for t in range(4):
+                nc.tensor.transpose(yt[:, t, :], y_sbs[i][:, t:512:4], ident[:])
+            y_turned[i] = yt
+
+        def y_out(i):
+            yt = y_turned[i]
+            y_grp = work.tile([P, 128, 4], BF16, align_bytes=64, name="y_grp")
+            nc.scalar.copy(out=y_grp[:], in_=yt[:].rearrange("p t r -> p r t"))
+            y_groups[i] = y_grp
+
+        def y_quant(i):
+            m = slice(128 * i, 128 * (i + 1))
+            nc.vector.quantize_mx(
+                out=y_codes[:, m].bitcast(FP8X4), scales=y_scales[:, m], in_=y_groups[i][:].rearrange("p r t -> p (r t)")
+            )
+            nc.sync.dma_start(
+                out=out_1[0].rearrange("p m t -> p (m t)")[:, 512 * i : 512 * (i + 1)].bitcast(I32), in_=y_codes[:, m].bitcast(I32)
+            )
+            if i % 4 == 3:
+                h = slice(128 * (i - 3), 128 * (i + 1))
+                for q in range(4):
+                    nc.sync.dma_start(
+                        out=out_2[0][4 * q : 4 * q + 4, h].bitcast(I32), in_=y_scales[32 * q : 32 * q + 4, h].bitcast(I32)
+                    )
+
+        x_turn(0)
+        x_out(0)
+        w_perm(0)
+        x_quant(0)
+        u_mm(0)
+        make_gains()
+        s_square(0)
+        s_third(0)
+        x_turn(1)
+        x_out(1)
+        x_quant(1)
+        w_perm(1)
+        u_mm(1)
+
+        def c_steps(m, engine):
+            for j, at in C_STEP.items():
+                if at == m:
+                    for h in range(2):
+                        if C_ENGINE[j][h] == engine:
+                            c_interleave(j, h)
+
+        steps = 2 * TILES
+        c_steps(-1, "V")
+        c_steps(-1, "S")
+
+        def y_chain(j):
+            y_mm(j)
+            v_y(j)
+            y_turn(j)
+            y_out(j)
+            y_quant(j)
+
+        for n in range(steps):
+            i, odd = divmod(n, 2)
+            k_tiles(n)
+            if n + 1 < steps:
+                s_square(n + 1)
+            v_k2(n)
+            if n in K1S:
+                s_k1(n)
+            else:
+                v_k1(n)
+            for j, at in C_STEP.items():
+                if at + 1 == n:
+                    c_quant(j)
+            c_steps(n, "V")
+            c_steps(n, "S")
+            if n in K1S:
+                s_k1b(n)
+            if n + 1 < steps:
+                s_third(n + 1)
+            v_k3(n)
+            if n + 2 < steps:
+                u_mm(n + 2)
+            if odd == 0 and i + 2 < TILES:
+                x_turn(i + 2)
+                x_out(i + 2)
+            if odd and i + 2 < TILES:
+                x_quant(i + 2)
+            if n in Y_AT:
+                y_chain(Y_AT[n])
+            if odd:
+                k_quant(i)
+
+        y_chain(TILES - 1)

@@ -20,24 +20,25 @@ ACT = mybir.ActivationFunctionType
 P = 128
 TILES = N // P
 
-C_ENGINE = ["VS","VS","VS","VS","SS","SS"]
-C_STEP = {0: -1, 1: -1, 2: 1, 3: 4, 4: 2, 5: 4}
-K1S = {7, 8, 10, 12, 13, 14}
+C_ENGINE = ["VS","VS","GS","VS","SS","SG"]
+C_STEP = {0: 0, 1: -1, 2: 2, 3: 4, 4: 3, 5: 4}
+K1S = {1, 4, 6, 7, 8, 9, 10, 11, 12, 14, 15}
+ZG = {0, 1, 3, 5, 6, 7, 8, 9, 10, 11, 13, 15}
 Y_STEP = {}
-Y_AT = {5: 0, 7: 1, 8: 2, 9: 3, 10: 4, 12: 5, 15: 6}
+Y_AT = {5: 0, 7: 1, 8: 2, 10: 3, 11: 4, 12: 5, 15: 6}
 
 
 def tile_hermitechaosridgeexpansiondegreethree_x2_kernel(tc, x, w_words, w_scales, g, c, b, out_0, out_1, out_2):
     nc = tc.nc
     with ExitStack() as ctx:
         keep = ctx.enter_context(tc.tile_pool(name="keep", bufs=1))
-        work = ctx.enter_context(tc.tile_pool(name="work", bufs=3))
+        work = ctx.enter_context(tc.tile_pool(name="work", bufs=5))
         psum = ctx.enter_context(tc.psum_pool(name="psum", bufs=1))
 
         ident = keep.tile([P, P], F32, align_bytes=64, name="ident")
         g_rows = keep.tile([P, 512], BF16, align_bytes=64, name="g_rows")
         g_perm = keep.tile([P, 4, 128], F32, align_bytes=64, name="g_perm")
-        gains = keep.tile([P, 4, 2, 4], F32, align_bytes=64, name="gains")
+        gains = keep.tile([P, 3, 2, 4], F32, align_bytes=64, name="gains")
         ws_raw = keep.tile([P, 2, 1024], U8, align_bytes=64, name="ws_raw")
         ws = keep.tile([P, 2, 2, 4, 128], U8, align_bytes=64, name="ws")
         w_raw = keep.tile([P, 2, 2, 1024], U8, align_bytes=64, name="w_raw")
@@ -52,8 +53,8 @@ def tile_hermitechaosridgeexpansiondegreethree_x2_kernel(tc, x, w_words, w_scale
         y_scales = keep.tile([P, N], U8, align_bytes=64, name="y_scales")
         warm = keep.tile([P, 1], F32, align_bytes=64, name="warm")
 
-        nc.vector.memset(g_rows[:].bitcast(I32), 0)
         nc.vector.memset(ws_raw[:].rearrange("p g n -> p (g n)").bitcast(I32), 0)
+        nc.vector.memset(g_rows[:].bitcast(I32), 0)
         nc.sync.dma_start(out=g_rows[0:6, :], in_=g.rearrange("d (h f) -> (d h) f", h=2))
         xs = []
         for i in range(TILES):
@@ -91,9 +92,9 @@ def tile_hermitechaosridgeexpansiondegreethree_x2_kernel(tc, x, w_words, w_scale
         load_x(3)
         load_c(4)
         load_c(5)
-        nc.sync.dma_start(out=bias[:], in_=b.partition_broadcast(P))
         for i in range(4, TILES):
             load_x(i)
+        nc.sync.dma_start(out=bias[:], in_=b.partition_broadcast(P))
 
         make_identity(nc, ident[:])
         nc.vector.memset(warm[:], 0.0)
@@ -103,12 +104,12 @@ def tile_hermitechaosridgeexpansiondegreethree_x2_kernel(tc, x, w_words, w_scale
             out=g_perm[:].rearrange("p t (B e) -> p t B e", e=8),
             in_=g_rows[:].rearrange("p (B t e) -> p t B e", t=4, e=8),
         )
-        gt = psum.tile([P, 4, 128], F32, tag="turn", bufs=2, name="gt")
+        gt = psum.tile([P, 4, 128], F32, tag="gt", bufs=1, name="gt")
         for t in range(4):
             nc.tensor.transpose(gt[:, t, :], g_perm[:, t, :], ident[:])
 
         def make_gains():
-          for k, (d, f) in enumerate([(0, 1.0), (1, 1.0 / math.sqrt(2.0)), (2, 1.0 / math.sqrt(6.0)), (2, -3.0 / math.sqrt(6.0))]):
+          for k, (d, f) in enumerate([(0, 1.0), (2, 1.0 / math.sqrt(3.0)), (2, -3.0 / math.sqrt(6.0))]):
               nc.vector.tensor_scalar_mul(gains[:, k, :, :], gt[:, :, 2 * d : 2 * d + 2].rearrange("p t r -> p r t"), f)
 
         x_groups = {}
@@ -153,7 +154,7 @@ def tile_hermitechaosridgeexpansiondegreethree_x2_kernel(tc, x, w_words, w_scale
         c_groups = {}
 
         def c_interleave(j, h):
-                if h == 0:
+                if j not in c_groups:
                     c_grp_new = work.tile([P, 512, 4], BF16, align_bytes=64, name="c_grp_new")
                     c_groups[j] = c_grp_new
                 c_grp = c_groups[j]
@@ -198,11 +199,14 @@ def tile_hermitechaosridgeexpansiondegreethree_x2_kernel(tc, x, w_words, w_scale
 
         def s_k1b(n):
             i, fg = divmod(n, 2)
-            nc.scalar.copy(out=ka[i][:, fg, 0, :, :], in_=k1_slots[n][:].rearrange("p t n -> p n t"))
+            nc.scalar.copy(
+                out=ka[i][:, fg, 0, :, :].rearrange("p (c i) t -> p c t i", i=4),
+                in_=k1_slots[n][:].rearrange("p t (c i) -> p c t i", i=4),
+            )
 
         def u_mm(n):
             i, fg = divmod(n, 2)
-            u = psum.tile([P, 4, 128], F32, tag="u", bufs=4, name="u")
+            u = psum.tile([P, 4, 128], F32, tag="u", bufs=3, name="u")
             for t in range(4):
                 for kg in range(2):
                     nc.tensor.matmul_mx(
@@ -217,20 +221,21 @@ def tile_hermitechaosridgeexpansiondegreethree_x2_kernel(tc, x, w_words, w_scale
             u_banks[n] = u
 
         def s_square(n):
-            u2 = work.tile([P, 4, 128], F32, align_bytes=64, name="u2")
-            nc.scalar.activation(out=u2[:], in_=u_banks[n][:], func=ACT.Square)
+            u2 = work.tile([P, 128, 4], F32, align_bytes=64, name="u2")
+            nc.scalar.activation(out=u2[:], in_=u_banks[n][:].rearrange("p t n -> p n t"), func=ACT.Square, scale=2.0**-0.25)
             squares[n] = u2
 
         def s_third(n):
             z = work.tile([P, 4, 128], F32, align_bytes=64, name="z")
             for t in range(4):
-                nc.scalar.activation(
-                    out=z[:, t, :],
-                    in_=squares[n][:, t, :],
-                    func=ACT.Identity,
-                    scale=gains[:, 2, n % 2, t : t + 1],
-                    bias=gains[:, 3, n % 2, t : t + 1],
-                )
+                a3 = gains[:, 1, n % 2, t : t + 1]
+                b3 = gains[:, 2, n % 2, t : t + 1]
+                if n in ZG:
+                    nc.gpsimd.tensor_scalar(
+                        out=z[:, t, :], in0=squares[n][:, :, t], scalar1=a3, scalar2=b3, op0=ALU.mult, op1=ALU.add
+                    )
+                else:
+                    nc.scalar.activation(out=z[:, t, :], in_=squares[n][:, :, t], func=ACT.Identity, scale=a3, bias=b3)
             thirds[n] = z
 
         def spread(k, fg):
@@ -248,9 +253,9 @@ def tile_hermitechaosridgeexpansiondegreethree_x2_kernel(tc, x, w_words, w_scale
             i, fg = divmod(n, 2)
             nc.vector.scalar_tensor_tensor(
                 out=ka[i][:, fg, 1, :, :],
-                in0=squares[n][:].rearrange("p t n -> p n t"),
-                scalar=-1.0,
-                in1=spread(1, fg),
+                in0=squares[n][:],
+                scalar=-1.0 / math.sqrt(2.0),
+                in1=gt[:, :, 2 + fg].unsqueeze(1).to_broadcast([P, 128, 4]),
                 op0=ALU.add,
                 op1=ALU.mult,
             )
@@ -264,9 +269,9 @@ def tile_hermitechaosridgeexpansiondegreethree_x2_kernel(tc, x, w_words, w_scale
         def v_k3(n):
             i, fg = divmod(n, 2)
             nc.vector.tensor_tensor(
-                out=kb[i][:, fg, :, :],
-                in0=u_banks[n][:].rearrange("p t n -> p n t"),
-                in1=thirds[n][:].rearrange("p t n -> p n t"),
+                out=kb[i][:, fg, :, :].rearrange("p (c i) t -> p c t i", i=4),
+                in0=u_banks[n][:].rearrange("p t (c i) -> p c t i", i=4),
+                in1=thirds[n][:].rearrange("p t (c i) -> p c t i", i=4),
                 op=ALU.mult,
             )
 
@@ -366,6 +371,7 @@ def tile_hermitechaosridgeexpansiondegreethree_x2_kernel(tc, x, w_words, w_scale
                             c_interleave(j, h)
 
         steps = 2 * TILES
+        c_steps(-1, "G")
         c_steps(-1, "V")
         c_steps(-1, "S")
 
@@ -389,6 +395,7 @@ def tile_hermitechaosridgeexpansiondegreethree_x2_kernel(tc, x, w_words, w_scale
             for j, at in C_STEP.items():
                 if at + 1 == n:
                     c_quant(j)
+            c_steps(n, "G")
             c_steps(n, "V")
             c_steps(n, "S")
             if n in K1S:

@@ -20,12 +20,14 @@ ACT = mybir.ActivationFunctionType
 P = 128
 TILES = N // P
 
-C_ENGINE = ["VS","VS","GS","VS","SS","SG"]
-C_STEP = {0: 0, 1: -1, 2: 2, 3: 4, 4: 3, 5: 4}
-K1S = {1, 4, 6, 7, 8, 9, 10, 11, 12, 14, 15}
-ZG = {0, 1, 3, 5, 6, 7, 8, 9, 10, 11, 13, 15}
-Y_STEP = {}
-Y_AT = {5: 0, 7: 1, 8: 2, 10: 3, 11: 4, 12: 5, 15: 6}
+C_ENGINE = ['VS', 'VS', 'GS', 'VS', 'SS', 'SG']
+C_STEP = {0: -1, 1: 0, 2: 1, 3: 1, 4: 3, 5: 5}
+K1S = {1, 2, 6, 7, 9, 10, 11, 13, 14, 15}
+ZG = {0, 1, 2, 3, 4, 5, 6, 9, 10, 11, 12, 13, 14, 15}
+CASTV = {7}
+OUTV = ()
+OFF = (2, 3, 4)
+Y_AT = {6: 0, 7: 1, 8: 2, 9: 3, 12: 4, 14: 5, 15: 6}
 
 
 def tile_hermitechaosridgeexpansiondegreethree_x2_kernel(tc, x, w_words, w_scales, g, c, b, out_0, out_1, out_2):
@@ -186,6 +188,7 @@ def tile_hermitechaosridgeexpansiondegreethree_x2_kernel(tc, x, w_words, w_scale
         y_sbs = {}
         y_groups = {}
         y_turned = {}
+        y_halves = {}
         k1_slots = {}
 
         def s_k1(n):
@@ -243,7 +246,7 @@ def tile_hermitechaosridgeexpansiondegreethree_x2_kernel(tc, x, w_words, w_scale
 
         def k_tiles(n):
             i, fg = divmod(n, 2)
-            if fg == 0:
+            if fg == 0 and i not in ka:
                 ka_t = work.tile([P, 2, 2, 128, 4], BF16, align_bytes=64, name="ka_t")
                 kb_t = work.tile([P, 2, 128, 4], BF16, align_bytes=64, name="kb_t")
                 ka[i] = ka_t
@@ -322,22 +325,35 @@ def tile_hermitechaosridgeexpansiondegreethree_x2_kernel(tc, x, w_words, w_scale
             nc.sync.dma_start(out=out_0[128 * i : 128 * (i + 1), :], in_=y_sb[:])
             y_sbs[i] = y_sb
 
+        def y_cast(i):
+            y_half = work.tile([P, 512], BF16, align_bytes=64, name="y_half")
+            if i in CASTV:
+                nc.vector.tensor_copy(out=y_half[:], in_=y_sbs[i][:])
+            else:
+                nc.scalar.copy(out=y_half[:], in_=y_sbs[i][:])
+            y_halves[i] = y_half
+
         def y_turn(i):
-            yt = psum.tile([P, 4, 128], F32, tag="turn", bufs=2, name="yt")
-            for t in range(4):
-                nc.tensor.transpose(yt[:, t, :], y_sbs[i][:, t:512:4], ident[:])
+            words = y_halves[i][:].bitcast(F32)
+            yt = psum.tile([P, 2, 128], F32, tag="turn", bufs=2, name="yt")
+            for u in range(2):
+                nc.tensor.transpose(yt[:, u, :], words[:, u:256:2], ident[:])
             y_turned[i] = yt
 
         def y_out(i):
             yt = y_turned[i]
-            y_grp = work.tile([P, 128, 4], BF16, align_bytes=64, name="y_grp")
-            nc.scalar.copy(out=y_grp[:], in_=yt[:].rearrange("p t r -> p r t"))
+            y_grp = work.tile([P, 512], BF16, align_bytes=64, name="y_grp")
+            out, in_ = y_grp[:].bitcast(F32).rearrange("p (r u) -> p r u", u=2), yt[:].rearrange("p u r -> p r u")
+            if i in OUTV:
+                nc.vector.tensor_copy(out=out, in_=in_)
+            else:
+                nc.scalar.copy(out=out, in_=in_)
             y_groups[i] = y_grp
 
         def y_quant(i):
             m = slice(128 * i, 128 * (i + 1))
             nc.vector.quantize_mx(
-                out=y_codes[:, m].bitcast(FP8X4), scales=y_scales[:, m], in_=y_groups[i][:].rearrange("p r t -> p (r t)")
+                out=y_codes[:, m].bitcast(FP8X4), scales=y_scales[:, m], in_=y_groups[i][:]
             )
             nc.sync.dma_start(
                 out=out_1[0].rearrange("p m t -> p (m t)")[:, 512 * i : 512 * (i + 1)].bitcast(I32), in_=y_codes[:, m].bitcast(I32)
@@ -349,20 +365,6 @@ def tile_hermitechaosridgeexpansiondegreethree_x2_kernel(tc, x, w_words, w_scale
                         out=out_2[0][4 * q : 4 * q + 4, h].bitcast(I32), in_=y_scales[32 * q : 32 * q + 4, h].bitcast(I32)
                     )
 
-        x_turn(0)
-        x_out(0)
-        w_perm(0)
-        x_quant(0)
-        u_mm(0)
-        make_gains()
-        s_square(0)
-        s_third(0)
-        x_turn(1)
-        x_out(1)
-        x_quant(1)
-        w_perm(1)
-        u_mm(1)
-
         def c_steps(m, engine):
             for j, at in C_STEP.items():
                 if at == m:
@@ -370,49 +372,87 @@ def tile_hermitechaosridgeexpansiondegreethree_x2_kernel(tc, x, w_words, w_scale
                         if C_ENGINE[j][h] == engine:
                             c_interleave(j, h)
 
+        x_turn(0)
+        x_out(0)
+        w_perm(0)
+        x_quant(0)
+        x_turn(1)
+        x_out(1)
+        u_mm(0)
+        make_gains()
+        s_square(0)
+        w_perm(1)
+        s_third(0)
+        x_quant(1)
+        u_mm(1)
+        for e in "GSV":
+            c_steps(-1, e)
+
         steps = 2 * TILES
-        c_steps(-1, "G")
-        c_steps(-1, "V")
-        c_steps(-1, "S")
-
-        def y_chain(j):
-            y_mm(j)
-            v_y(j)
-            y_turn(j)
-            y_out(j)
-            y_quant(j)
-
         for n in range(steps):
             i, odd = divmod(n, 2)
             k_tiles(n)
+            if not odd and i + 2 < TILES:
+                x_turn(i + 2)
+            if n - OFF[1] in Y_AT:
+                y_turn(Y_AT[n - OFF[1]])
+            if n + 2 < steps:
+                u_mm(n + 2)
             if n + 1 < steps:
                 s_square(n + 1)
+            if not odd and i + 2 < TILES:
+                x_out(i + 2)
+            if n - OFF[1] in Y_AT:
+                y_out(Y_AT[n - OFF[1]])
             v_k2(n)
+            if odd == 0 and i > 0:
+                k_quant(i - 1)
             if n in K1S:
-                s_k1(n)
+                pass
             else:
                 v_k1(n)
             for j, at in C_STEP.items():
                 if at + 1 == n:
                     c_quant(j)
-            c_steps(n, "G")
-            c_steps(n, "V")
-            c_steps(n, "S")
-            if n in K1S:
-                s_k1b(n)
+            if n in Y_AT:
+                y_mm(Y_AT[n])
+            if n - OFF[0] in Y_AT:
+                v_y(Y_AT[n - OFF[0]])
+                y_cast(Y_AT[n - OFF[0]])
+            for e in "GSV":
+                c_steps(n, e)
             if n + 1 < steps:
                 s_third(n + 1)
+                if n + 1 in K1S:
+                    if odd:
+                        k_tiles(n + 1)
+                    s_k1(n + 1)
+                    s_k1b(n + 1)
             v_k3(n)
-            if n + 2 < steps:
-                u_mm(n + 2)
-            if odd == 0 and i + 2 < TILES:
-                x_turn(i + 2)
-                x_out(i + 2)
             if odd and i + 2 < TILES:
                 x_quant(i + 2)
-            if n in Y_AT:
-                y_chain(Y_AT[n])
-            if odd:
-                k_quant(i)
+            if n - OFF[2] in Y_AT:
+                y_quant(Y_AT[n - OFF[2]])
 
-        y_chain(TILES - 1)
+        last = TILES - 1
+        k_quant(last)
+        y_mm(last)
+        at = {j: s for s, j in Y_AT.items()}
+        rest = [j for j in range(last)]
+        for stage in range(3):
+            for j in rest:
+                if at[j] + OFF[stage] >= steps:
+                    if stage == 0:
+                        v_y(j)
+                        y_cast(j)
+                    elif stage == 1:
+                        y_turn(j)
+                        y_out(j)
+                    elif j < last - 1:
+                        y_quant(j)
+        v_y(last)
+        y_cast(last)
+        y_quant(last - 1)
+        y_turn(last)
+        y_out(last)
+        y_quant(last)

@@ -20,14 +20,15 @@ ACT = mybir.ActivationFunctionType
 P = 128
 TILES = N // P
 
-C_ENGINE = ['VS', 'VS', 'GS', 'VS', 'SS', 'SG']
-C_STEP = {0: -1, 1: 0, 2: 1, 3: 1, 4: 3, 5: 5}
-K1S = {1, 2, 6, 7, 9, 10, 11, 13, 14, 15}
-ZG = {0, 1, 2, 3, 4, 5, 6, 9, 10, 11, 12, 13, 14, 15}
-CASTV = {7}
-OUTV = ()
-OFF = (2, 3, 4)
-Y_AT = {6: 0, 7: 1, 8: 2, 9: 3, 12: 4, 14: 5, 15: 6}
+C_ENGINE = ['SV', 'VS', 'VS', 'VG', 'SS', 'VG']
+C_STEP = {0: -1, 1: -1, 2: -1, 3: 1, 4: 5, 5: 4}
+K1S = {3, 7, 9, 11, 13, 15}
+ZG = ()
+CASTV = {4, 7}
+OUTV = {7}
+WORDS = True
+OFF = (2, 4, 5)
+Y_AT = {6: 0, 7: 1, 8: 2, 10: 3, 11: 4, 14: 5, 15: 6}
 
 
 def tile_hermitechaosridgeexpansiondegreethree_x2_kernel(tc, x, w_words, w_scales, g, c, b, out_0, out_1, out_2):
@@ -326,6 +327,8 @@ def tile_hermitechaosridgeexpansiondegreethree_x2_kernel(tc, x, w_words, w_scale
             y_sbs[i] = y_sb
 
         def y_cast(i):
+            if not WORDS:
+                return
             y_half = work.tile([P, 512], BF16, align_bytes=64, name="y_half")
             if i in CASTV:
                 nc.vector.tensor_copy(out=y_half[:], in_=y_sbs[i][:])
@@ -334,6 +337,12 @@ def tile_hermitechaosridgeexpansiondegreethree_x2_kernel(tc, x, w_words, w_scale
             y_halves[i] = y_half
 
         def y_turn(i):
+            if not WORDS:
+                yt = psum.tile([P, 4, 128], F32, tag="turn", bufs=2, name="yt")
+                for t in range(4):
+                    nc.tensor.transpose(yt[:, t, :], y_sbs[i][:, t:512:4], ident[:])
+                y_turned[i] = yt
+                return
             words = y_halves[i][:].bitcast(F32)
             yt = psum.tile([P, 2, 128], F32, tag="turn", bufs=2, name="yt")
             for u in range(2):
@@ -343,7 +352,10 @@ def tile_hermitechaosridgeexpansiondegreethree_x2_kernel(tc, x, w_words, w_scale
         def y_out(i):
             yt = y_turned[i]
             y_grp = work.tile([P, 512], BF16, align_bytes=64, name="y_grp")
-            out, in_ = y_grp[:].bitcast(F32).rearrange("p (r u) -> p r u", u=2), yt[:].rearrange("p u r -> p r u")
+            if WORDS:
+              out, in_ = y_grp[:].bitcast(F32).rearrange("p (r u) -> p r u", u=2), yt[:].rearrange("p u r -> p r u")
+            else:
+              out, in_ = y_grp[:].rearrange("p (r t) -> p r t", t=4), yt[:].rearrange("p t r -> p r t")
             if i in OUTV:
                 nc.vector.tensor_copy(out=out, in_=in_)
             else:

@@ -20,15 +20,15 @@ ACT = mybir.ActivationFunctionType
 P = 128
 TILES = N // P
 
-C_ENGINE = ['SV', 'VS', 'VS', 'VG', 'SS', 'VG']
-C_STEP = {0: -1, 1: -1, 2: -1, 3: 1, 4: 5, 5: 4}
-K1S = {3, 7, 9, 11, 13, 15}
+C_ENGINE = ['SV', 'VS', 'VS', 'SG', 'SS', 'VS']
+C_STEP = {0: -1, 1: -1, 2: -1, 3: 2, 4: 5, 5: 4}
+K1S = {7, 9, 11, 12, 13}
 ZG = ()
 CASTV = {4, 7}
 OUTV = {7}
-WORDS = True
+WORDS = False
 OFF = (2, 4, 5)
-Y_AT = {6: 0, 7: 1, 8: 2, 10: 3, 11: 4, 14: 5, 15: 6}
+Y_AT = {6: 0, 7: 1, 9: 2, 10: 3, 11: 4, 14: 5, 15: 6}
 
 
 def tile_hermitechaosridgeexpansiondegreethree_x2_kernel(tc, x, w_words, w_scales, g, c, b, out_0, out_1, out_2):
@@ -225,8 +225,8 @@ def tile_hermitechaosridgeexpansiondegreethree_x2_kernel(tc, x, w_words, w_scale
             u_banks[n] = u
 
         def s_square(n):
-            u2 = work.tile([P, 128, 4], F32, align_bytes=64, name="u2")
-            nc.scalar.activation(out=u2[:], in_=u_banks[n][:].rearrange("p t n -> p n t"), func=ACT.Square, scale=2.0**-0.25)
+            u2 = work.tile([P, 4, 128], F32, align_bytes=64, name="u2")
+            nc.scalar.activation(out=u2[:], in_=u_banks[n][:], func=ACT.Square, scale=2.0**-0.25)
             squares[n] = u2
 
         def s_third(n):
@@ -236,10 +236,10 @@ def tile_hermitechaosridgeexpansiondegreethree_x2_kernel(tc, x, w_words, w_scale
                 b3 = gains[:, 2, n % 2, t : t + 1]
                 if n in ZG:
                     nc.gpsimd.tensor_scalar(
-                        out=z[:, t, :], in0=squares[n][:, :, t], scalar1=a3, scalar2=b3, op0=ALU.mult, op1=ALU.add
+                        out=z[:, t, :], in0=squares[n][:, t, :], scalar1=a3, scalar2=b3, op0=ALU.mult, op1=ALU.add
                     )
                 else:
-                    nc.scalar.activation(out=z[:, t, :], in_=squares[n][:, :, t], func=ACT.Identity, scale=a3, bias=b3)
+                    nc.scalar.activation(out=z[:, t, :], in_=squares[n][:, t, :], func=ACT.Identity, scale=a3, bias=b3)
             thirds[n] = z
 
         def spread(k, fg):
@@ -257,7 +257,7 @@ def tile_hermitechaosridgeexpansiondegreethree_x2_kernel(tc, x, w_words, w_scale
             i, fg = divmod(n, 2)
             nc.vector.scalar_tensor_tensor(
                 out=ka[i][:, fg, 1, :, :],
-                in0=squares[n][:],
+                in0=squares[n][:].rearrange("p t n -> p n t"),
                 scalar=-1.0 / math.sqrt(2.0),
                 in1=gt[:, :, 2 + fg].unsqueeze(1).to_broadcast([P, 128, 4]),
                 op0=ALU.add,
@@ -419,6 +419,10 @@ def tile_hermitechaosridgeexpansiondegreethree_x2_kernel(tc, x, w_words, w_scale
             v_k2(n)
             if odd == 0 and i > 0:
                 k_quant(i - 1)
+            if n == steps - 1:
+                k_codes_tiles(i)
+                k_quant_part(i, 0, 2, ka[i][:, 0, :, :, :].rearrange("p d n t -> p (d n t)"))
+                k_quant_part(i, 4, 5, kb[i][:, 0, :, :].rearrange("p n t -> p (n t)"))
             if n in K1S:
                 pass
             else:
@@ -440,15 +444,18 @@ def tile_hermitechaosridgeexpansiondegreethree_x2_kernel(tc, x, w_words, w_scale
                         k_tiles(n + 1)
                     s_k1(n + 1)
                     s_k1b(n + 1)
+            if n == steps - 1:
+                k_quant_part(i, 2, 4, ka[i][:, 1, :, :, :].rearrange("p d n t -> p (d n t)"))
             v_k3(n)
+            if n == steps - 1:
+                k_quant_part(i, 5, 6, kb[i][:, 1, :, :].rearrange("p n t -> p (n t)"))
+                y_mm(i)
             if odd and i + 2 < TILES:
                 x_quant(i + 2)
             if n - OFF[2] in Y_AT:
                 y_quant(Y_AT[n - OFF[2]])
 
         last = TILES - 1
-        k_quant(last)
-        y_mm(last)
         at = {j: s for s, j in Y_AT.items()}
         rest = [j for j in range(last)]
         for stage in range(3):

import math
from contextlib import ExitStack

import concourse.mybir as mybir
from concourse.masks import make_identity

N, D, F, O = 1024, 1024, 1024, 512
FLOPS = 2 * N * D * F + 3 * 2 * N * F * O

F32 = mybir.dt.float32
BF16 = mybir.dt.bfloat16
U32 = mybir.dt.uint32
I32 = mybir.dt.int32
U8 = mybir.dt.uint8
FP8X4 = mybir.dt.float8_e4m3fn_x4
FP4X4 = mybir.dt.float4_e2m1fn_x4
ALU = mybir.AluOpType
ACT = mybir.ActivationFunctionType

P = 128
TILES = N // P

C_ENGINE = ['SV', 'VS', 'VS', 'SG', 'SS', 'VS']
C_STEP = {0: -1, 1: -1, 2: -1, 3: 2, 4: 5, 5: 4}
K1S = {7, 9, 11, 12, 13}
ZG = ()
CASTV = {4, 7}
OUTV = {7}
WORDS = False
OFF = (2, 4, 5)
Y_AT = {6: 0, 7: 1, 9: 2, 10: 3, 11: 4, 14: 5, 15: 6}


def tile_hermitechaosridgeexpansiondegreethree_x2_kernel(tc, x, w_words, w_scales, g, c, b, out_0, out_1, out_2):
    nc = tc.nc
    with ExitStack() as ctx:
        keep = ctx.enter_context(tc.tile_pool(name="keep", bufs=1))
        work = ctx.enter_context(tc.tile_pool(name="work", bufs=5))
        psum = ctx.enter_context(tc.psum_pool(name="psum", bufs=1))

        ident = keep.tile([P, P], F32, align_bytes=64, name="ident")
        g_rows = keep.tile([P, 512], BF16, align_bytes=64, name="g_rows")
        g_perm = keep.tile([P, 4, 128], F32, align_bytes=64, name="g_perm")
        gains = keep.tile([P, 3, 2, 4], F32, align_bytes=64, name="gains")
        ws_raw = keep.tile([P, 2, 1024], U8, align_bytes=64, name="ws_raw")
        ws = keep.tile([P, 2, 2, 4, 128], U8, align_bytes=64, name="ws")
        w_raw = keep.tile([P, 2, 2, 1024], U8, align_bytes=64, name="w_raw")
        wc = keep.tile([P, 2, 2, 4, 256], U8, align_bytes=64, name="wc")
        x_codes = keep.tile([P, TILES, 2, 128], U32, align_bytes=64, name="x_codes")
        x_scales = keep.tile([P, TILES, 2, 128], U8, align_bytes=64, name="x_scales")
        c_raw = keep.tile([P, 6, 4, 512], BF16, align_bytes=64, name="c_raw")
        c_codes = keep.tile([P, 6, 512], U32, align_bytes=64, name="c_codes")
        c_scales = keep.tile([P, 6, 512], U8, align_bytes=64, name="c_scales")
        bias = keep.tile([P, 512], BF16, align_bytes=64, name="bias")
        y_codes = keep.tile([P, N], U32, align_bytes=64, name="y_codes")
        y_scales = keep.tile([P, N], U8, align_bytes=64, name="y_scales")
        warm = keep.tile([P, 1], F32, align_bytes=64, name="warm")

        nc.vector.memset(ws_raw[:].rearrange("p g n -> p (g n)").bitcast(I32), 0)
        nc.vector.memset(g_rows[:].bitcast(I32), 0)
        nc.sync.dma_start(out=g_rows[0:6, :], in_=g.rearrange("d (h f) -> (d h) f", h=2))
        xs = []
        for i in range(TILES):
            x_sb = keep.tile([P, D], BF16, align_bytes=64, name="x_sb%d" % i)
            xs.append(x_sb)

        def load_x(i):
            nc.sync.dma_start(out=xs[i][:], in_=x[128 * i : 128 * (i + 1), :])

        def load_c(j):
            rows = c[j // 2, 512 * (j % 2) : 512 * (j % 2 + 1), :].rearrange("(B t e) o -> t B e o", t=4, e=8)
            for t in range(4):
                nc.sync.dma_start(out=c_raw[:, j, t, :], in_=rows[t])

        def load_w(fg):
            half = slice(1024 * fg, 1024 * (fg + 1))
            nc.sync.dma_start(
                out=w_raw[:, fg, :, :].bitcast(I32), in_=w_words[:, :, half].rearrange("g p n -> p g n").bitcast(I32)
            )

        load_x(0)
        load_w(0)
        for q in range(4):
            nc.scalar.dma_start(
                out=ws_raw[32 * q : 32 * q + 4, :, :].bitcast(I32),
                in_=w_scales[:, 4 * q : 4 * q + 4, :].rearrange("g q n -> q g n").bitcast(I32),
            )
        load_x(1)
        load_w(1)
        load_c(0)
        load_c(1)
        load_x(2)
        load_c(2)
        load_c(3)
        load_x(3)
        load_c(4)
        load_c(5)
        for i in range(4, TILES):
            load_x(i)
        nc.sync.dma_start(out=bias[:], in_=b.partition_broadcast(P))

        make_identity(nc, ident[:])
        nc.vector.memset(warm[:], 0.0)
        nc.scalar.activation(out=warm[:], in_=warm[:], func=ACT.Square)

        nc.vector.tensor_copy(
            out=g_perm[:].rearrange("p t (B e) -> p t B e", e=8),
            in_=g_rows[:].rearrange("p (B t e) -> p t B e", t=4, e=8),
        )
        gt = psum.tile([P, 4, 128], F32, tag="gt", bufs=1, name="gt")
        for t in range(4):
            nc.tensor.transpose(gt[:, t, :], g_perm[:, t, :], ident[:])

        def make_gains():
          for k, (d, f) in enumerate([(0, 1.0), (2, 1.0 / math.sqrt(3.0)), (2, -3.0 / math.sqrt(6.0))]):
              nc.vector.tensor_scalar_mul(gains[:, k, :, :], gt[:, :, 2 * d : 2 * d + 2].rearrange("p t r -> p r t"), f)

        x_groups = {}

        x_banks = {}

        def x_turn(i):
            words = xs[i][:].bitcast(F32)
            xt = psum.tile([P, 4, 128], F32, tag="turn", bufs=2, name="xt")
            for kg in range(2):
                for u in range(2):
                    nc.tensor.transpose(xt[:, 2 * kg + u, :], words[:, 256 * kg + u : 256 * (kg + 1) : 2], ident[:])
            x_banks[i] = xt

        def x_out(i):
            xt = x_banks[i]
            x_grp = work.tile([P, 2 * 128 * 4], BF16, align_bytes=64, name="x_grp")
            nc.scalar.copy(
                out=x_grp[:].bitcast(F32).rearrange("p (k r u) -> p k r u", k=2, u=2),
                in_=xt[:].rearrange("p (k u) r -> p k r u", u=2),
            )
            x_groups[i] = x_grp

        def x_quant(i):
            nc.vector.quantize_mx(
                out=x_codes[:, i, :, :].rearrange("p k n -> p (k n)").bitcast(FP8X4),
                scales=x_scales[:, i, :, :].rearrange("p k n -> p (k n)"),
                in_=x_groups[i][:],
            )

        def w_perm(fg):
            for kg in range(2):
                nc.vector.tensor_copy(
                    out=wc[:, fg, kg, :, :].bitcast(I32).rearrange("p t (B e) -> p t B e", e=4),
                    in_=w_raw[:, fg, kg, :].bitcast(I32).rearrange("p (B t e) -> p t B e", t=4, e=4),
                )
                nc.vector.tensor_copy(
                    out=ws[:, fg, kg, :, :].bitcast(I32).rearrange("p t (B e) -> p t B e", e=2),
                    in_=ws_raw[:, kg, 512 * fg : 512 * (fg + 1)].bitcast(I32).rearrange("p (B t e) -> p t B e", t=4, e=2),
                )

        c_groups = {}

        def c_interleave(j, h):
                if j not in c_groups:
                    c_grp_new = work.tile([P, 512, 4], BF16, align_bytes=64, name="c_grp_new")
                    c_groups[j] = c_grp_new
                c_grp = c_groups[j]
                o = slice(256 * h, 256 * (h + 1))
                dst = c_grp[:, o, :].rearrange("p (c i) t -> p c t i", i=4)
                src = c_raw[:, j, :, o].rearrange("p t (c i) -> p c t i", i=4)
                who = C_ENGINE[j][h]
                if who == "V":
                    nc.vector.tensor_copy(out=dst, in_=src)
                elif who == "S":
                    nc.scalar.copy(out=dst, in_=src)
                else:
                    nc.gpsimd.tensor_scalar(out=dst, in0=src, scalar1=1.0, scalar2=0.0, op0=ALU.mult, op1=ALU.add)

        def c_quant(j):
            nc.vector.quantize_mx(
                out=c_codes[:, j, :].bitcast(FP8X4),
                scales=c_scales[:, j, :],
                in_=c_groups[j][:].rearrange("p o t -> p (o t)"),
            )

        u_banks = {}
        squares = {}
        thirds = {}
        ka = {}
        kb = {}
        k_codes = {}
        y_banks = {}
        y_sbs = {}
        y_groups = {}
        y_turned = {}
        y_halves = {}
        k1_slots = {}

        def s_k1(n):
            fg = n % 2
            k1_slot = work.tile([P, 4, 128], BF16, align_bytes=64, name="k1_slot")
            for t in range(4):
                nc.scalar.activation(
                    out=k1_slot[:, t, :], in_=u_banks[n][:, t, :], func=ACT.Copy, scale=gains[:, 0, fg, t : t + 1]
                )
            k1_slots[n] = k1_slot

        def s_k1b(n):
            i, fg = divmod(n, 2)
            nc.scalar.copy(
                out=ka[i][:, fg, 0, :, :].rearrange("p (c i) t -> p c t i", i=4),
                in_=k1_slots[n][:].rearrange("p t (c i) -> p c t i", i=4),
            )

        def u_mm(n):
            i, fg = divmod(n, 2)
            u = psum.tile([P, 4, 128], F32, tag="u", bufs=3, name="u")
            for t in range(4):
                for kg in range(2):
                    nc.tensor.matmul_mx(
                        out=u[:, t, :],
                        lhsT=wc[:, fg, kg, t, :].bitcast(FP4X4),
                        lhsT_scale=ws[:, fg, kg, t, :],
                        rhs=x_codes[:, i, kg, :].bitcast(FP8X4),
                        rhs_scale=x_scales[:, i, kg, :],
                        start=(kg == 0),
                        stop=(kg == 1),
                    )
            u_banks[n] = u

        def s_square(n):
            u2 = work.tile([P, 4, 128], F32, align_bytes=64, name="u2")
            nc.scalar.activation(out=u2[:], in_=u_banks[n][:], func=ACT.Square, scale=2.0**-0.25)
            squares[n] = u2

        def s_third(n):
            z = work.tile([P, 4, 128], F32, align_bytes=64, name="z")
            for t in range(4):
                a3 = gains[:, 1, n % 2, t : t + 1]
                b3 = gains[:, 2, n % 2, t : t + 1]
                if n in ZG:
                    nc.gpsimd.tensor_scalar(
                        out=z[:, t, :], in0=squares[n][:, t, :], scalar1=a3, scalar2=b3, op0=ALU.mult, op1=ALU.add
                    )
                else:
                    nc.scalar.activation(out=z[:, t, :], in_=squares[n][:, t, :], func=ACT.Identity, scale=a3, bias=b3)
            thirds[n] = z

        def spread(k, fg):
            return gains[:, k, fg, :].unsqueeze(1).to_broadcast([P, 128, 4])

        def k_tiles(n):
            i, fg = divmod(n, 2)
            if fg == 0 and i not in ka:
                ka_t = work.tile([P, 2, 2, 128, 4], BF16, align_bytes=64, name="ka_t")
                kb_t = work.tile([P, 2, 128, 4], BF16, align_bytes=64, name="kb_t")
                ka[i] = ka_t
                kb[i] = kb_t

        def v_k2(n):
            i, fg = divmod(n, 2)
            nc.vector.scalar_tensor_tensor(
                out=ka[i][:, fg, 1, :, :],
                in0=squares[n][:].rearrange("p t n -> p n t"),
                scalar=-1.0 / math.sqrt(2.0),
                in1=gt[:, :, 2 + fg].unsqueeze(1).to_broadcast([P, 128, 4]),
                op0=ALU.add,
                op1=ALU.mult,
            )

        def v_k1(n):
            i, fg = divmod(n, 2)
            nc.vector.tensor_tensor(
                out=ka[i][:, fg, 0, :, :], in0=u_banks[n][:].rearrange("p t n -> p n t"), in1=spread(0, fg), op=ALU.mult
            )

        def v_k3(n):
            i, fg = divmod(n, 2)
            nc.vector.tensor_tensor(
                out=kb[i][:, fg, :, :].rearrange("p (c i) t -> p c t i", i=4),
                in0=u_banks[n][:].rearrange("p t (c i) -> p c t i", i=4),
                in1=thirds[n][:].rearrange("p t (c i) -> p c t i", i=4),
                op=ALU.mult,
            )

        def k_codes_tiles(i):
            kc = keep.tile([P, 6, 128], U32, align_bytes=64, name="kc%d" % i)
            ks = keep.tile([P, 6, 128], U8, align_bytes=64, name="ks%d" % i)
            k_codes[i] = (kc, ks)

        def k_quant_part(i, a, z, src):
            kc, ks = k_codes[i]
            nc.vector.quantize_mx(
                out=kc[:, a:z, :].rearrange("p j n -> p (j n)").bitcast(FP8X4),
                scales=ks[:, a:z, :].rearrange("p j n -> p (j n)"),
                in_=src,
            )

        def k_quant(i):
            k_codes_tiles(i)
            k_quant_part(i, 0, 4, ka[i][:].rearrange("p f d n t -> p (f d n t)"))
            k_quant_part(i, 4, 6, kb[i][:].rearrange("p f n t -> p (f n t)"))

        def y_pass(i, a, j, s):
            kc, ks = k_codes[i]
            nc.tensor.matmul_mx(
                out=y_banks[i][:],
                lhsT=kc[:, s, :].bitcast(FP8X4),
                lhsT_scale=ks[:, s, :],
                rhs=c_codes[:, j, :].bitcast(FP8X4),
                rhs_scale=c_scales[:, j, :],
                start=(a == 0),
                stop=(a == 5),
            )

        def y_bank(i):
            y = psum.tile([P, 512], F32, tag="y", bufs=2, name="y")
            y_banks[i] = y

        PASSES = [(0, 0), (2, 1), (4, 4), (1, 2), (3, 3), (5, 5)]

        def y_mm(i):
            y_bank(i)
            for a, (j, s) in enumerate(PASSES):
                y_pass(i, a, j, s)

        def v_y(i):
            y_sb = work.tile([P, 512], F32, align_bytes=64, name="y_sb")
            nc.vector.tensor_tensor(out=y_sb[:], in0=y_banks[i][:], in1=bias[:], op=ALU.add)
            nc.sync.dma_start(out=out_0[128 * i : 128 * (i + 1), :], in_=y_sb[:])
            y_sbs[i] = y_sb

        def y_cast(i):
            if not WORDS:
                return
            y_half = work.tile([P, 512], BF16, align_bytes=64, name="y_half")
            if i in CASTV:
                nc.vector.tensor_copy(out=y_half[:], in_=y_sbs[i][:])
            else:
                nc.scalar.copy(out=y_half[:], in_=y_sbs[i][:])
            y_halves[i] = y_half

        def y_turn(i):
            if not WORDS:
                yt = psum.tile([P, 4, 128], F32, tag="turn", bufs=2, name="yt")
                for t in range(4):
                    nc.tensor.transpose(yt[:, t, :], y_sbs[i][:, t:512:4], ident[:])
                y_turned[i] = yt
                return
            words = y_halves[i][:].bitcast(F32)
            yt = psum.tile([P, 2, 128], F32, tag="turn", bufs=2, name="yt")
            for u in range(2):
                nc.tensor.transpose(yt[:, u, :], words[:, u:256:2], ident[:])
            y_turned[i] = yt

        def y_out(i):
            yt = y_turned[i]
            y_grp = work.tile([P, 512], BF16, align_bytes=64, name="y_grp")
            if WORDS:
              out, in_ = y_grp[:].bitcast(F32).rearrange("p (r u) -> p r u", u=2), yt[:].rearrange("p u r -> p r u")
            else:
              out, in_ = y_grp[:].rearrange("p (r t) -> p r t", t=4), yt[:].rearrange("p t r -> p r t")
            if i in OUTV:
                nc.vector.tensor_copy(out=out, in_=in_)
            else:
                nc.scalar.copy(out=out, in_=in_)
            y_groups[i] = y_grp

        def y_quant(i):
            m = slice(128 * i, 128 * (i + 1))
            nc.vector.quantize_mx(
                out=y_codes[:, m].bitcast(FP8X4), scales=y_scales[:, m], in_=y_groups[i][:]
            )
            nc.sync.dma_start(
                out=out_1[0].rearrange("p m t -> p (m t)")[:, 512 * i : 512 * (i + 1)].bitcast(I32), in_=y_codes[:, m].bitcast(I32)
            )
            if i % 4 == 3:
                h = slice(128 * (i - 3), 128 * (i + 1))
                for q in range(4):
                    nc.sync.dma_start(
                        out=out_2[0][4 * q : 4 * q + 4, h].bitcast(I32), in_=y_scales[32 * q : 32 * q + 4, h].bitcast(I32)
                    )

        def c_steps(m, engine):
            for j, at in C_STEP.items():
                if at == m:
                    for h in range(2):
                        if C_ENGINE[j][h] == engine:
                            c_interleave(j, h)

        x_turn(0)
        x_out(0)
        w_perm(0)
        x_quant(0)
        x_turn(1)
        x_out(1)
        u_mm(0)
        make_gains()
        s_square(0)
        w_perm(1)
        s_third(0)
        x_quant(1)
        u_mm(1)
        for e in "GSV":
            c_steps(-1, e)

        steps = 2 * TILES
        for n in range(steps):
            i, odd = divmod(n, 2)
            k_tiles(n)
            if not odd and i + 2 < TILES:
                x_turn(i + 2)
            if n - OFF[1] in Y_AT:
                y_turn(Y_AT[n - OFF[1]])
            if n + 2 < steps:
                u_mm(n + 2)
            if n + 1 < steps:
                s_square(n + 1)
            if not odd and i + 2 < TILES:
                x_out(i + 2)
            if n - OFF[1] in Y_AT:
                y_out(Y_AT[n - OFF[1]])
            v_k2(n)
            if odd == 0 and i > 0:
                k_quant(i - 1)
            if n == steps - 1:
                k_codes_tiles(i)
                k_quant_part(i, 0, 2, ka[i][:, 0, :, :, :].rearrange("p d n t -> p (d n t)"))
                k_quant_part(i, 4, 5, kb[i][:, 0, :, :].rearrange("p n t -> p (n t)"))
            if n in K1S:
                pass
            else:
                v_k1(n)
            for j, at in C_STEP.items():
                if at + 1 == n:
                    c_quant(j)
            if n in Y_AT:
                y_mm(Y_AT[n])
            if n - OFF[0] in Y_AT:
                v_y(Y_AT[n - OFF[0]])
                y_cast(Y_AT[n - OFF[0]])
            for e in "GSV":
                c_steps(n, e)
            if n + 1 < steps:
                s_third(n + 1)
                if n + 1 in K1S:
                    if odd:
                        k_tiles(n + 1)
                    s_k1(n + 1)
                    s_k1b(n + 1)
            if n == steps - 1:
                k_quant_part(i, 2, 4, ka[i][:, 1, :, :, :].rearrange("p d n t -> p (d n t)"))
            v_k3(n)
            if n == steps - 1:
                k_quant_part(i, 5, 6, kb[i][:, 1, :, :].rearrange("p n t -> p (n t)"))
                y_mm(i)
            if odd and i + 2 < TILES:
                x_quant(i + 2)
            if n - OFF[2] in Y_AT:
                y_quant(Y_AT[n - OFF[2]])

        last = TILES - 1
        at = {j: s for s, j in Y_AT.items()}
        rest = [j for j in range(last)]
        for stage in range(3):
            for j in rest:
                if at[j] + OFF[stage] >= steps:
                    if stage == 0:
                        v_y(j)
                        y_cast(j)
                    elif stage == 1:
                        y_turn(j)
                        y_out(j)
                    elif j < last - 1:
                        y_quant(j)
        v_y(last)
        y_cast(last)
        y_quant(last - 1)
        y_turn(last)
        y_out(last)
        y_quant(last)
